import numpy as np
import ml_dtypes


def mxq(x, axis, fmt="e4m3"):
    dtype, down = {"e4m3": (ml_dtypes.float8_e4m3fn, 7), "e5m2": (ml_dtypes.float8_e5m2, 14)}[fmt]
    v = np.moveaxis(np.asarray(x, np.float32).astype(ml_dtypes.bfloat16).astype(np.float64), axis, -1)
    blocks = v.reshape(v.shape[:-1] + (-1, 32))
    amax = np.abs(blocks).max(-1, keepdims=True)
    byte = np.maximum(np.where(amax > 0, np.frexp(amax)[1] - 1 + 127, 0) - down, 1)
    scale = np.exp2(byte - 127.0)
    codes = (blocks / scale).astype(np.float32).astype(dtype).astype(np.float64)
    return np.moveaxis((codes * scale).reshape(v.shape), -1, axis)


WIDE = False


def mx_kscale(k):
    if not WIDE:
        return np.ones(k)
    levels = np.array([10, -10, 5, -5, 0])
    if k % 512:
        return np.exp2(np.random.permutation(np.resize(levels, k // 32))).repeat(32)
    a = np.empty((k // 512, 16))
    for p in range(k // 512):
        a[p, :8] = np.random.permutation(np.resize(levels, 8))
        for g in range(8):
            far = levels[np.abs(levels - a[p, g]) >= 10]
            a[p, g + 8] = far[np.random.randint(len(far))]
    return np.exp2(a.ravel()).repeat(32)


def f64(x):
    return np.asarray(x).astype(np.float64)


def striped(idx):
    return np.tile(idx.reshape(-1, 16).T, (8, 1)).astype(np.uint16)


def unstriped(offs):
    return offs[:16].T.reshape(-1).astype(np.int64)


E2M1 = np.array([0.0, 0.5, 1.0, 1.5, 2.0, 3.0, 4.0, 6.0, -0.0, -0.5, -1.0, -1.5, -2.0, -3.0, -4.0, -6.0])


def pack_weight(w, fmt):
    k, n = w.shape
    w = f64(np.asarray(w, np.float32).astype(ml_dtypes.bfloat16)).reshape(k // 32, 32, n)
    amax = np.abs(w).max(1)
    if fmt == "e4m3":
        byte = np.frexp(amax)[1] - 1 + 127 - 7
    else:
        mant, ex = np.frexp(amax / 6.0)
        byte = np.where(mant > 0.5, ex, ex - 1) + 127
    byte = np.clip(np.where(amax > 0, byte, 1), 1, 254)
    scaled = (w * np.exp2(127.0 - byte)[:, None, :]).reshape(k, n).astype(np.float32)
    by_word = np.ascontiguousarray(scaled.reshape(k // 512, 128, 4, n).transpose(0, 1, 3, 2))
    if fmt == "e4m3":
        words = by_word.astype(ml_dtypes.float8_e4m3fn).view(np.uint8)
    else:
        c = by_word.astype(ml_dtypes.float4_e2m1fn).view(np.uint8) & 0xF
        words = (c[..., 0::2] | (c[..., 1::2] << 4)).reshape(k // 512, 128, 2 * n)
    return np.ascontiguousarray(words), np.ascontiguousarray(byte.astype(np.uint8).reshape(k // 512, 16, n))


def unpack_weight(words, scales, fmt):
    g, _, n = scales.shape
    words = np.ascontiguousarray(words).reshape(g, 128, n, -1)
    if fmt == "e4m3":
        vals = words.view(ml_dtypes.float8_e4m3fn).astype(np.float64)
    else:
        nib = np.empty((g, 128, n, 4), np.uint8)
        nib[..., 0::2] = words & 0xF
        nib[..., 1::2] = words >> 4
        vals = E2M1[nib]
    vals = vals * np.repeat(np.exp2(scales.astype(np.float64) - 127.0), 8, axis=1)[..., None]
    return vals.transpose(0, 1, 3, 2).reshape(g * 512, n)


def gelu(v):
    return 0.5 * v * (1.0 + np.tanh(np.sqrt(2.0 / np.pi) * (v + 0.044715 * v**3)))


K, H, T, S, T3, S2, P = 1024, 1024, 4096, 1024, 2048, 512, 512


def setup_inputs():
    n = np.random.standard_normal
    s = mx_kscale(K)[:, None]
    u = mx_kscale(H)[:, None]
    d = {}
    d["tab_words"], d["tab_scales"] = pack_weight(n((K, T)) * s, "e4m3")
    d["tab2_words"], d["tab2_scales"] = pack_weight(n((H, T3)) / u / H**0.5, "e4m3")
    d["w1"] = (0.9 * n((K, H)) / K**0.5 / s).astype(np.float32)
    d["w4_words"], d["w4_scales"] = pack_weight(0.9 * n((K, H)) / K**0.5 / s, "e2m1")
    d["gain"] = (np.exp(0.3 * n(H)) * u[:, 0]).astype(np.float32)
    d["shell"] = np.exp(0.3 * n(S2)).astype(np.float32)
    d["offs"] = striped(np.random.permutation(T)[:S])
    d["offs2"] = striped(np.random.permutation(T3)[:S2])
    d["pos1"] = striped(np.random.permutation(S)[:P])
    d["pos2"] = striped(np.random.permutation(S)[:P])
    return d


def reference(tab_words, tab_scales, tab2_words, tab2_scales, w1, w4_words, w4_scales,
              gain, shell, offs, offs2, pos1, pos2):
    v = unpack_weight(tab_words, tab_scales, "e4m3")[:, unstriped(offs)]
    v2 = unpack_weight(tab2_words, tab2_scales, "e4m3")[:, unstriped(offs2)]
    w4 = unpack_weight(w4_words, w4_scales, "e2m1")
    a = mxq(f64(w1), 0, "e4m3").T @ v
    b = w4.T @ v
    h = (a * b + a + b) * f64(gain)[:, None]
    e = np.abs(v2.T @ mxq(h, 0, "e4m3"))
    launch = e[:, unstriped(pos1)]
    burst = e[:, unstriped(pos2)]
    return np.maximum(launch, burst) * f64(shell)[:, None]

@@ -1,0 +1,196 @@
+from contextlib import ExitStack
+
+import concourse.mybir as mybir
+
+K, H, T, S, T3, S2, NP = 1024, 1024, 4096, 1024, 2048, 512, 512
+FLOPS = 2 * K * H * S * 2 + 2 * H * S2 * S
+
+F32 = mybir.dt.float32
+BF16 = mybir.dt.bfloat16
+I32 = mybir.dt.int32
+U32 = mybir.dt.uint32
+U16 = mybir.dt.uint16
+U8 = mybir.dt.uint8
+FP8X4 = mybir.dt.float8_e4m3fn_x4
+FP4X4 = mybir.dt.float4_e2m1fn_x4
+ACT = mybir.ActivationFunctionType
+ALU = mybir.AluOpType
+
+P = 128
+PACK = 4
+KP = 512
+NT = 512
+
+
+def tile_list_firework_shell_scores_kernel(
+    tc, tab_words, tab_scales, tab2_words, tab2_scales, w1, w4_words, w4_scales,
+    gain, shell, offs, offs2, pos1, pos2, out,
+):
+    nc = tc.nc
+    with ExitStack() as ctx:
+        keep = ctx.enter_context(tc.tile_pool(name="keep", bufs=1))
+        ring = ctx.enter_context(tc.tile_pool(name="ring", bufs=2))
+        psum = ctx.enter_context(tc.psum_pool(name="psum", bufs=1))
+
+        def kept(shape, dtype, name):
+            return keep.tile(shape, dtype, name=name, align_bytes=64)
+
+        offs_sb = kept([P, S // 16], U16, "offs_sb")
+        offs2_sb = kept([P, S2 // 16], U16, "offs2_sb")
+        pos1_sb = kept([P, NP // 16], U16, "pos1_sb")
+        pos2_sb = kept([P, NP // 16], U16, "pos2_sb")
+        tabw = [kept([P, T], I32, "tabw%d" % a) for a in range(2)]
+        tabs = kept([P, 2 * T], U8, "tabs")
+        tab2w = [kept([P, T3], I32, "tab2w%d" % a) for a in range(2)]
+        tab2s = kept([P, T3], U8, "tab2s")
+        w4w_raw = kept([P, 2 * 2 * H], U8, "w4w_raw")
+        w4s_raw = kept([P, 2 * H], U8, "w4s_raw")
+        w4w = kept([P, 2 * 2 * H], U8, "w4w")
+        w4s = kept([P, 2 * H], U8, "w4s")
+        gain_sb = kept([P, 2, PACK], F32, "gain_sb")
+        shell_sb = kept([P, S2 // P], F32, "shell_sb")
+        w1raw = {(b, a): kept([P, PACK, KP], F32, "w1raw%d%d" % (b, a)) for b in range(2) for a in range(2)}
+
+        def load_w1(b, a):
+            rows = w1[a * KP:(a + 1) * KP, b * KP:(b + 1) * KP]
+            nc.sync.dma_start(out=w1raw[b, a][:], in_=rows.rearrange("(p j) c -> p j c", j=PACK))
+
+        def load_words(tile, words):
+            nc.sync.dma_start(out=tile[:], in_=words.rearrange("p t i -> p (t i)").bitcast(I32))
+
+        def load_side_by_side(queue, tile, scales):
+            for q in range(4):
+                queue.dma_start(
+                    out=tile[32 * q:32 * q + 4, :].bitcast(I32).rearrange("r (a c) -> r a c", a=2),
+                    in_=scales[:, 4 * q:4 * q + 4, :].bitcast(I32).rearrange("a r c -> r a c"))
+
+        nc.vector.memset(tabs[:].bitcast(I32), 0)
+        nc.gpsimd.memset(w4s_raw[:].bitcast(I32), 0)
+        nc.gpsimd.memset(tab2s[:].bitcast(I32), 0)
+
+        nc.sync.dma_start(offs_sb[:], offs)
+        nc.sync.dma_start(out=w4w_raw[:].bitcast(I32).rearrange("p (a c) -> p a c", a=2),
+                          in_=w4_words.bitcast(I32).rearrange("a p c -> p a c"))
+        load_words(tabw[0], tab_words[0])
+        load_w1(0, 0)
+        load_side_by_side(nc.scalar, tabs, tab_scales)
+        load_side_by_side(nc.gpsimd, w4s_raw, w4_scales)
+        for q in range(4):
+            nc.gpsimd.dma_start(out=tab2s[32 * q:32 * q + 8, :].bitcast(I32),
+                                in_=tab2_scales[:, 4 * q:4 * q + 4, :].bitcast(I32))
+        nc.gpsimd.dma_start(out=gain_sb[:], in_=gain.rearrange("(b p t) -> p b t", b=2, t=PACK))
+        with nc.allow_non_contiguous_dma(reason="one factor a partition"):
+            nc.gpsimd.dma_start(out=shell_sb[:], in_=shell.rearrange("(m p) -> p m", p=P))
+        load_w1(0, 1)
+        nc.sync.dma_start(offs2_sb[:], offs2)
+        load_words(tabw[1], tab_words[1])
+        load_w1(1, 0)
+        load_w1(1, 1)
+        load_words(tab2w[0], tab2_words[0])
+        load_words(tab2w[1], tab2_words[1])
+        nc.sync.dma_start(pos1_sb[:], pos1)
+        nc.sync.dma_start(pos2_sb[:], pos2)
+
+        nc.vector.tensor_copy(
+            out=w4w[:].bitcast(U16).rearrange("p (g t m) -> p g m t", t=PACK, m=P),
+            in_=w4w_raw[:].bitcast(U16).rearrange("p (g m t) -> p g m t", t=PACK, m=P))
+        nc.vector.tensor_copy(
+            out=w4s[:].rearrange("p (g t m) -> p g m t", t=PACK, m=P),
+            in_=w4s_raw[:].rearrange("p (g m t) -> p g m t", t=PACK, m=P))
+
+        vw = {(a, jh): kept([P, NT], U32, "vw%d%d" % (a, jh)) for a in range(2) for jh in range(2)}
+        vs = [kept([P, S], U8, "vs%d" % a) for a in range(2)]
+        v2w = [kept([P, S2], U32, "v2w%d" % a) for a in range(2)]
+        v2s = kept([P, S2], U8, "v2s")
+
+        def gather_v(a, jh):
+            nc.vector.tensor_copy(vw[a, jh][:], tabw[a][:].bitcast(U32).indirect(offs_sb[:, 32 * jh:32 * jh + 32]))
+
+        w1q = {}
+
+        def quantize_w1(b, a):
+            grouped = ring.tile([P, KP * PACK], BF16, name="w1g", align_bytes=64)
+            nc.scalar.copy(out=grouped[:].rearrange("p (t m j) -> p m j t", t=PACK, j=PACK),
+                           in_=w1raw[b, a][:].rearrange("p j (m t) -> p m j t", t=PACK))
+            codes = kept([P, KP], U32, "w1c%d%d" % (b, a))
+            scales = kept([P, KP], U8, "w1s%d%d" % (b, a))
+            nc.vector.quantize_mx(out=codes[:].bitcast(FP8X4), scales=scales[:], in_=grouped[:])
+            w1q[b, a] = (codes, scales)
+
+        for a in range(2):
+            nc.vector.tensor_copy(vs[a][:], tabs[:, a * T:(a + 1) * T].indirect(offs_sb[:]))
+        gather_v(0, 0)
+        gather_v(0, 1)
+        nc.vector.tensor_copy(v2s[:], tab2s[:].indirect(offs2_sb[:]))
+        quantize_w1(0, 0)
+        quantize_w1(0, 1)
+        gather_v(1, 0)
+        gather_v(1, 1)
+
+        hq = {}
+
+        def stage1(b, jh):
+            gb = ring.tile([P, PACK, NT], F32, name="gb")
+            prod = ring.tile([P, PACK, NT], F32, name="prod")
+            cols = slice(jh * NT, (jh + 1) * NT)
+            for t in range(PACK):
+                acc_b = psum.tile([P, NT], F32, name="acc_b", bufs=3)
+                acc_a = psum.tile([P, NT], F32, name="acc_a", bufs=3)
+                for a in range(2):
+                    c0 = a * H + b * KP + t * P
+                    nc.tensor.matmul_mx(
+                        out=acc_b[:], lhsT=w4w[:, 2 * c0:2 * c0 + 2 * P].bitcast(FP4X4), lhsT_scale=w4s[:, c0:c0 + P],
+                        rhs=vw[a, jh][:].bitcast(FP8X4), rhs_scale=vs[a][:, cols], start=(a == 0), stop=(a == 1))
+                for a in range(2):
+                    codes, scales = w1q[b, a]
+                    nc.tensor.matmul_mx(
+                        out=acc_a[:], lhsT=codes[:, t * P:(t + 1) * P].bitcast(FP8X4),
+                        lhsT_scale=scales[:, t * P:(t + 1) * P],
+                        rhs=vw[a, jh][:].bitcast(FP8X4), rhs_scale=vs[a][:, cols], start=(a == 0), stop=(a == 1))
+                g = gain_sb[:, b, t:t + 1]
+                nc.scalar.activation(out=gb[:, t, :], in_=acc_b[:], func=ACT.Copy, scale=g)
+                nc.vector.scalar_tensor_tensor(out=prod[:, t, :], in0=gb[:, t, :], scalar=g, in1=acc_a[:],
+                                               op0=ALU.add, op1=ALU.mult)
+            hb = ring.tile([P, NT * PACK], BF16, name="hb", align_bytes=64)
+            nc.vector.tensor_tensor(
+                out=hb[:].rearrange("p (c i t) -> p c t i", i=4, t=PACK),
+                in0=prod[:].rearrange("p t (c i) -> p c t i", i=4),
+                in1=gb[:].rearrange("p t (c i) -> p c t i", i=4), op=ALU.add)
+            codes = kept([P, NT], U32, "hc%d%d" % (b, jh))
+            scales = kept([P, NT], U8, "hs%d%d" % (b, jh))
+            nc.vector.quantize_mx(out=codes[:].bitcast(FP8X4), scales=scales[:], in_=hb[:])
+            hq[b, jh] = (codes, scales)
+
+        e = [kept([P, S], F32, "e%d" % m) for m in range(S2 // P)]
+
+        def stage2(m, jh):
+            acc_e = psum.tile([P, NT], F32, name="acc_e", bufs=2)
+            for b in range(2):
+                codes, scales = hq[b, jh]
+                nc.tensor.matmul_mx(
+                    out=acc_e[:], lhsT=v2w[b][:, m * P:(m + 1) * P].bitcast(FP8X4),
+                    lhsT_scale=v2s[4 * b:P, m * P:(m + 1) * P],
+                    rhs=codes[:].bitcast(FP8X4), rhs_scale=scales[:], start=(b == 0), stop=(b == 1))
+            nc.scalar.activation(out=e[m][:, jh * NT:(jh + 1) * NT], in_=acc_e[:], func=ACT.Abs)
+
+        stage1(0, 0)
+        quantize_w1(1, 0)
+        quantize_w1(1, 1)
+        stage1(0, 1)
+        for b in range(2):
+            nc.vector.tensor_copy(v2w[b][:], tab2w[b][:].bitcast(U32).indirect(offs2_sb[:]))
+        stage1(1, 0)
+        for m in range(S2 // P):
+            stage2(m, 0)
+        stage1(1, 1)
+        for m in range(S2 // P):
+            stage2(m, 1)
+            launch = ring.tile([P, NP], F32, name="launch")
+            burst = ring.tile([P, NP], F32, name="burst")
+            nc.vector.tensor_copy(launch[:], e[m][:].indirect(pos1_sb[:]))
+            nc.vector.tensor_copy(burst[:], e[m][:].indirect(pos2_sb[:]))
+            larger = ring.tile([P, NP], F32, name="larger")
+            nc.vector.tensor_tensor(out=larger[:], in0=launch[:], in1=burst[:], op=ALU.max)
+            result = ring.tile([P, NP], F32, name="result")
+            nc.scalar.activation(out=result[:], in_=larger[:], func=ACT.Copy, scale=shell_sb[:, m:m + 1])
+            nc.sync.dma_start(out=out[m * P:(m + 1) * P, :], in_=result[:])

@@ -40,7 +40,7 @@ def tile_list_firework_shell_scores_kernel(
         pos1_sb = kept([P, NP // 16], U16, "pos1_sb")
         pos2_sb = kept([P, NP // 16], U16, "pos2_sb")
         tabw = [kept([P, T], I32, "tabw%d" % a) for a in range(2)]
-        tabs = kept([P, 2 * T], U8, "tabs")
+        tabs = kept([P, T], U8, "tabs")
         tab2w = [kept([P, T3], I32, "tab2w%d" % a) for a in range(2)]
         tab2s = kept([P, T3], U8, "tab2s")
         w4w_raw = kept([P, 2 * 2 * H], U8, "w4w_raw")
@@ -64,43 +64,44 @@ def tile_list_firework_shell_scores_kernel(
                     out=tile[32 * q:32 * q + 4, :].bitcast(I32).rearrange("r (a c) -> r a c", a=2),
                     in_=scales[:, 4 * q:4 * q + 4, :].bitcast(I32).rearrange("a r c -> r a c"))
 
-        nc.vector.memset(tabs[:].bitcast(I32), 0)
-        nc.gpsimd.memset(w4s_raw[:].bitcast(I32), 0)
+        def load_packed(queue, tile, scales):
+            for q in range(4):
+                queue.dma_start(out=tile[32 * q:32 * q + 8, :].bitcast(I32),
+                                in_=scales[:, 4 * q:4 * q + 4, :].bitcast(I32))
+
+        vs = [kept([P, S], U8, "vs%d" % a) for a in range(2)]
+        nc.gpsimd.memset(tabs[:].bitcast(I32), 0)
+        nc.vector.memset(w4s_raw[:].bitcast(I32), 0)
         nc.gpsimd.memset(tab2s[:].bitcast(I32), 0)
+        nc.vector.memset(vs[1][:].bitcast(I32), 0)
 
         nc.sync.dma_start(offs_sb[:], offs)
+        nc.sync.dma_start(offs2_sb[:], offs2)
         nc.sync.dma_start(out=w4w_raw[:].bitcast(I32).rearrange("p (a c) -> p a c", a=2),
                           in_=w4_words.bitcast(I32).rearrange("a p c -> p a c"))
+        load_packed(nc.sync, tabs, tab_scales)
         load_words(tabw[0], tab_words[0])
         load_w1(0, 0)
-        load_side_by_side(nc.scalar, tabs, tab_scales)
-        load_side_by_side(nc.gpsimd, w4s_raw, w4_scales)
-        for q in range(4):
-            nc.gpsimd.dma_start(out=tab2s[32 * q:32 * q + 8, :].bitcast(I32),
-                                in_=tab2_scales[:, 4 * q:4 * q + 4, :].bitcast(I32))
-        nc.gpsimd.dma_start(out=gain_sb[:], in_=gain.rearrange("(b p t) -> p b t", b=2, t=PACK))
-        with nc.allow_non_contiguous_dma(reason="one factor a partition"):
-            nc.gpsimd.dma_start(out=shell_sb[:], in_=shell.rearrange("(m p) -> p m", p=P))
+        load_side_by_side(nc.sync, w4s_raw, w4_scales)
         load_w1(0, 1)
-        nc.sync.dma_start(offs2_sb[:], offs2)
+        load_packed(nc.sync, tab2s, tab2_scales)
         load_words(tabw[1], tab_words[1])
+        nc.sync.dma_start(out=gain_sb[:], in_=gain.rearrange("(b p t) -> p b t", b=2, t=PACK))
         load_w1(1, 0)
         load_w1(1, 1)
         load_words(tab2w[0], tab2_words[0])
         load_words(tab2w[1], tab2_words[1])
         nc.sync.dma_start(pos1_sb[:], pos1)
         nc.sync.dma_start(pos2_sb[:], pos2)
+        with nc.allow_non_contiguous_dma(reason="one factor a partition"):
+            nc.sync.dma_start(out=shell_sb[:], in_=shell.rearrange("(m p) -> p m", p=P))
 
         nc.vector.tensor_copy(
             out=w4w[:].bitcast(U16).rearrange("p (g t m) -> p g m t", t=PACK, m=P),
             in_=w4w_raw[:].bitcast(U16).rearrange("p (g m t) -> p g m t", t=PACK, m=P))
-        nc.vector.tensor_copy(
-            out=w4s[:].rearrange("p (g t m) -> p g m t", t=PACK, m=P),
-            in_=w4s_raw[:].rearrange("p (g m t) -> p g m t", t=PACK, m=P))
 
         vw = {(a, jh): kept([P, NT], U32, "vw%d%d" % (a, jh)) for a in range(2) for jh in range(2)}
-        vs = [kept([P, S], U8, "vs%d" % a) for a in range(2)]
-        v2w = [kept([P, S2], U32, "v2w%d" % a) for a in range(2)]
+        v2w = {(a, mh): kept([P, S2 // 2], U32, "v2w%d%d" % (a, mh)) for a in range(2) for mh in range(2)}
         v2s = kept([P, S2], U8, "v2s")
 
         def gather_v(a, jh):
@@ -117,10 +118,14 @@ def tile_list_firework_shell_scores_kernel(
             nc.vector.quantize_mx(out=codes[:].bitcast(FP8X4), scales=scales[:], in_=grouped[:])
             w1q[b, a] = (codes, scales)
 
-        for a in range(2):
-            nc.vector.tensor_copy(vs[a][:], tabs[:, a * T:(a + 1) * T].indirect(offs_sb[:]))
+        nc.vector.tensor_copy(vs[0][:], tabs[:].indirect(offs_sb[:]))
+        nc.scalar.dma_start(out=vs[1][0:112, :].bitcast(I32), in_=vs[0][4:116, :].bitcast(I32))
         gather_v(0, 0)
         gather_v(0, 1)
+        nc.vector.tensor_copy(
+            out=w4s[:].rearrange("p (g t m) -> p g m t", t=PACK, m=P),
+            in_=w4s_raw[:].rearrange("p (g m t) -> p g m t", t=PACK, m=P))
+
         nc.vector.tensor_copy(v2s[:], tab2s[:].indirect(offs2_sb[:]))
         quantize_w1(0, 0)
         quantize_w1(0, 1)
@@ -168,29 +173,46 @@ def tile_list_firework_shell_scores_kernel(
             for b in range(2):
                 codes, scales = hq[b, jh]
                 nc.tensor.matmul_mx(
-                    out=acc_e[:], lhsT=v2w[b][:, m * P:(m + 1) * P].bitcast(FP8X4),
+                    out=acc_e[:], lhsT=v2w[b, m // 2][:, (m % 2) * P:(m % 2 + 1) * P].bitcast(FP8X4),
                     lhsT_scale=v2s[4 * b:P, m * P:(m + 1) * P],
                     rhs=codes[:].bitcast(FP8X4), rhs_scale=scales[:], start=(b == 0), stop=(b == 1))
             nc.scalar.activation(out=e[m][:, jh * NT:(jh + 1) * NT], in_=acc_e[:], func=ACT.Abs)
+
+        def gather_v2(mh):
+            for b in range(2):
+                nc.vector.tensor_copy(v2w[b, mh][:],
+                                      tab2w[b][:].bitcast(U32).indirect(offs2_sb[:, 16 * mh:16 * mh + 16]))
+
+        def finish(m, n0, n1):
+            width = n1 - n0
+            launch = ring.tile([P, width], F32, name="launch")
+            burst = ring.tile([P, width], F32, name="burst")
+            nc.vector.tensor_copy(launch[:], e[m][:].indirect(pos1_sb[:, n0 // 16:n1 // 16]))
+            nc.vector.tensor_copy(burst[:], e[m][:].indirect(pos2_sb[:, n0 // 16:n1 // 16]))
+            larger = ring.tile([P, width], F32, name="larger")
+            nc.vector.tensor_tensor(out=larger[:], in0=launch[:], in1=burst[:], op=ALU.max)
+            result = ring.tile([P, width], F32, name="result")
+            nc.scalar.activation(out=result[:], in_=larger[:], func=ACT.Copy, scale=shell_sb[:, m:m + 1])
+            nc.sync.dma_start(out=out[m * P:(m + 1) * P, n0:n1], in_=result[:])
 
         stage1(0, 0)
         quantize_w1(1, 0)
         quantize_w1(1, 1)
         stage1(0, 1)
-        for b in range(2):
-            nc.vector.tensor_copy(v2w[b][:], tab2w[b][:].bitcast(U32).indirect(offs2_sb[:]))
         stage1(1, 0)
-        for m in range(S2 // P):
-            stage2(m, 0)
+        gather_v2(0)
+        stage2(0, 0)
+        stage2(1, 0)
         stage1(1, 1)
-        for m in range(S2 // P):
-            stage2(m, 1)
-            launch = ring.tile([P, NP], F32, name="launch")
-            burst = ring.tile([P, NP], F32, name="burst")
-            nc.vector.tensor_copy(launch[:], e[m][:].indirect(pos1_sb[:]))
-            nc.vector.tensor_copy(burst[:], e[m][:].indirect(pos2_sb[:]))
-            larger = ring.tile([P, NP], F32, name="larger")
-            nc.vector.tensor_tensor(out=larger[:], in0=launch[:], in1=burst[:], op=ALU.max)
-            result = ring.tile([P, NP], F32, name="result")
-            nc.scalar.activation(out=result[:], in_=larger[:], func=ACT.Copy, scale=shell_sb[:, m:m + 1])
-            nc.sync.dma_start(out=out[m * P:(m + 1) * P, :], in_=result[:])
+        gather_v2(1)
+        stage2(0, 1)
+        stage2(1, 1)
+        finish(0, 0, NP)
+        stage2(2, 0)
+        stage2(2, 1)
+        finish(1, 0, NP)
+        stage2(3, 0)
+        stage2(3, 1)
+        finish(2, 0, NP)
+        finish(3, 0, NP // 2)
+        finish(3, NP // 2, NP)

@@ -20,6 +20,7 @@ P = 128
 PACK = 4
 KP = 512
 NT = 512
+HALF = 256
 
 
 def tile_list_firework_shell_scores_kernel(
@@ -40,7 +41,7 @@ def tile_list_firework_shell_scores_kernel(
         pos1_sb = kept([P, NP // 16], U16, "pos1_sb")
         pos2_sb = kept([P, NP // 16], U16, "pos2_sb")
         tabw = [kept([P, T], I32, "tabw%d" % a) for a in range(2)]
-        tabs = kept([P, T], U8, "tabs")
+        tabs = kept([P, 2 * T], U8, "tabs")
         tab2w = [kept([P, T3], I32, "tab2w%d" % a) for a in range(2)]
         tab2s = kept([P, T3], U8, "tab2s")
         w4w_raw = kept([P, 2 * 2 * H], U8, "w4w_raw")
@@ -49,14 +50,18 @@ def tile_list_firework_shell_scores_kernel(
         w4s = kept([P, 2 * H], U8, "w4s")
         gain_sb = kept([P, 2, PACK], F32, "gain_sb")
         shell_sb = kept([P, S2 // P], F32, "shell_sb")
-        w1raw = {(b, a): kept([P, PACK, KP], F32, "w1raw%d%d" % (b, a)) for b in range(2) for a in range(2)}
+        w1raw = {(b, a, ch): keep.tile([P, PACK, HALF], F32, name="w1raw%d%d%d" % (b, a, ch),
+                                       tag="w1raw%d%d%d" % (b, a, ch), align_bytes=64)
+                 for b in range(2) for a in range(2) for ch in range(2)}
 
         def load_w1(b, a):
-            rows = w1[a * KP:(a + 1) * KP, b * KP:(b + 1) * KP]
-            nc.sync.dma_start(out=w1raw[b, a][:], in_=rows.rearrange("(p j) c -> p j c", j=PACK))
+            for ch in range(2):
+                c0 = b * KP + ch * HALF
+                rows = w1[a * KP:(a + 1) * KP, c0:c0 + HALF]
+                nc.sync.dma_start(out=w1raw[b, a, ch][:], in_=rows.rearrange("(p j) c -> p j c", j=PACK))
 
         def load_words(tile, words):
-            nc.sync.dma_start(out=tile[:], in_=words.rearrange("p t i -> p (t i)").bitcast(I32))
+            nc.sync.dma_start(out=tile, in_=words.rearrange("p t i -> p (t i)").bitcast(I32))
 
         def load_side_by_side(queue, tile, scales):
             for q in range(4):
@@ -70,27 +75,27 @@ def tile_list_firework_shell_scores_kernel(
                                 in_=scales[:, 4 * q:4 * q + 4, :].bitcast(I32))
 
         vs = [kept([P, S], U8, "vs%d" % a) for a in range(2)]
-        nc.gpsimd.memset(tabs[:].bitcast(I32), 0)
-        nc.vector.memset(w4s_raw[:].bitcast(I32), 0)
+        nc.gpsimd.memset(tabs[:, 0:T].bitcast(I32), 0)
+        nc.vector.memset(tabs[:, T:2 * T].bitcast(I32), 0)
+        nc.gpsimd.memset(w4s_raw[:].bitcast(I32), 0)
         nc.gpsimd.memset(tab2s[:].bitcast(I32), 0)
-        nc.vector.memset(vs[1][:].bitcast(I32), 0)
 
         nc.sync.dma_start(offs_sb[:], offs)
-        nc.sync.dma_start(offs2_sb[:], offs2)
+        nc.sync.dma_start(out=gain_sb[:], in_=gain.rearrange("(b p t) -> p b t", b=2, t=PACK))
         nc.sync.dma_start(out=w4w_raw[:].bitcast(I32).rearrange("p (a c) -> p a c", a=2),
                           in_=w4_words.bitcast(I32).rearrange("a p c -> p a c"))
-        load_packed(nc.sync, tabs, tab_scales)
-        load_words(tabw[0], tab_words[0])
+        load_side_by_side(nc.sync, tabs, tab_scales)
+        load_words(tabw[0][:], tab_words[0])
+        nc.sync.dma_start(offs2_sb[:], offs2)
+        load_packed(nc.gpsimd, tab2s, tab2_scales)
         load_w1(0, 0)
         load_side_by_side(nc.sync, w4s_raw, w4_scales)
+        load_words(tabw[1][:], tab_words[1])
         load_w1(0, 1)
-        load_packed(nc.sync, tab2s, tab2_scales)
-        load_words(tabw[1], tab_words[1])
-        nc.sync.dma_start(out=gain_sb[:], in_=gain.rearrange("(b p t) -> p b t", b=2, t=PACK))
         load_w1(1, 0)
         load_w1(1, 1)
-        load_words(tab2w[0], tab2_words[0])
-        load_words(tab2w[1], tab2_words[1])
+        load_words(tab2w[0][:], tab2_words[0])
+        load_words(tab2w[1][:], tab2_words[1])
         nc.sync.dma_start(pos1_sb[:], pos1)
         nc.sync.dma_start(pos2_sb[:], pos2)
         with nc.allow_non_contiguous_dma(reason="one factor a partition"):
@@ -101,7 +106,7 @@ def tile_list_firework_shell_scores_kernel(
             in_=w4w_raw[:].bitcast(U16).rearrange("p (g m t) -> p g m t", t=PACK, m=P))
 
         vw = {(a, jh): kept([P, NT], U32, "vw%d%d" % (a, jh)) for a in range(2) for jh in range(2)}
-        v2w = {(a, mh): kept([P, S2 // 2], U32, "v2w%d%d" % (a, mh)) for a in range(2) for mh in range(2)}
+        v2w = {}
         v2s = kept([P, S2], U8, "v2s")
 
         def gather_v(a, jh):
@@ -109,33 +114,42 @@ def tile_list_firework_shell_scores_kernel(
 
         w1q = {}
 
-        def quantize_w1(b, a):
-            grouped = ring.tile([P, KP * PACK], BF16, name="w1g", align_bytes=64)
-            nc.scalar.copy(out=grouped[:].rearrange("p (t m j) -> p m j t", t=PACK, j=PACK),
-                           in_=w1raw[b, a][:].rearrange("p j (m t) -> p m j t", t=PACK))
-            codes = kept([P, KP], U32, "w1c%d%d" % (b, a))
+        def quantize_w1(b, a, grouped, casts):
+            by_channel = grouped[:].rearrange("p (t m j) -> p m j t", t=PACK, j=PACK)
+            for ch in range(2):
+                casts[ch](out=by_channel[:, ch * 64:(ch + 1) * 64],
+                          in_=w1raw[b, a, ch][:].rearrange("p j (m t) -> p m j t", t=PACK))
+            codes = keep.tile([P, KP], U32, name="w1c%d%d" % (b, a), tag="w1c%d%d" % (b, a), align_bytes=64)
             scales = kept([P, KP], U8, "w1s%d%d" % (b, a))
             nc.vector.quantize_mx(out=codes[:].bitcast(FP8X4), scales=scales[:], in_=grouped[:])
             w1q[b, a] = (codes, scales)
 
-        nc.vector.tensor_copy(vs[0][:], tabs[:].indirect(offs_sb[:]))
-        nc.scalar.dma_start(out=vs[1][0:112, :].bitcast(I32), in_=vs[0][4:116, :].bitcast(I32))
+        for a in range(2):
+            nc.vector.tensor_copy(vs[a][:], tabs[:, a * T:(a + 1) * T].indirect(offs_sb[:]))
         gather_v(0, 0)
         gather_v(0, 1)
         nc.vector.tensor_copy(
             out=w4s[:].rearrange("p (g t m) -> p g m t", t=PACK, m=P),
             in_=w4s_raw[:].rearrange("p (g m t) -> p g m t", t=PACK, m=P))
-
+        on_scalar = (nc.scalar.copy, nc.scalar.copy)
+        quantize_w1(0, 0, ring.tile([P, KP * PACK], BF16, name="w1g", align_bytes=64), on_scalar)
         nc.vector.tensor_copy(v2s[:], tab2s[:].indirect(offs2_sb[:]))
-        quantize_w1(0, 0)
-        quantize_w1(0, 1)
         gather_v(1, 0)
         gather_v(1, 1)
+        quantize_w1(0, 1, keep.tile([P, KP * PACK], BF16, name="w1g01", tag="slot1", align_bytes=64),
+                    (nc.scalar.copy, nc.vector.tensor_copy))
 
         hq = {}
+        parts = {}
+        rounded = {}
+        groups = [(0, 0), (0, 1), (1, 0), (1, 1)]
+        gains = {}
+        for n, (b, jh) in enumerate(groups):
+            gains[b, jh] = keep.tile([P, PACK], F32, name="gains%d" % n, tag="slot%d" % n if n else "w1raw010", align_bytes=64)
+            nc.gpsimd.tensor_copy(gains[b, jh][:], gain_sb[:, b, :])
 
-        def stage1(b, jh):
-            gb = ring.tile([P, PACK, NT], F32, name="gb")
+        def products(b, jh):
+            gb = ring.tile([P, PACK, NT], F32, name="gb", bufs=3)
             prod = ring.tile([P, PACK, NT], F32, name="prod")
             cols = slice(jh * NT, (jh + 1) * NT)
             for t in range(PACK):
@@ -152,18 +166,24 @@ def tile_list_firework_shell_scores_kernel(
                         out=acc_a[:], lhsT=codes[:, t * P:(t + 1) * P].bitcast(FP8X4),
                         lhsT_scale=scales[:, t * P:(t + 1) * P],
                         rhs=vw[a, jh][:].bitcast(FP8X4), rhs_scale=vs[a][:, cols], start=(a == 0), stop=(a == 1))
-                g = gain_sb[:, b, t:t + 1]
+                g = gains[b, jh][:, t:t + 1]
                 nc.scalar.activation(out=gb[:, t, :], in_=acc_b[:], func=ACT.Copy, scale=g)
                 nc.vector.scalar_tensor_tensor(out=prod[:, t, :], in0=gb[:, t, :], scalar=g, in1=acc_a[:],
                                                op0=ALU.add, op1=ALU.mult)
-            hb = ring.tile([P, NT * PACK], BF16, name="hb", align_bytes=64)
-            nc.vector.tensor_tensor(
-                out=hb[:].rearrange("p (c i t) -> p c t i", i=4, t=PACK),
-                in0=prod[:].rearrange("p t (c i) -> p c t i", i=4),
-                in1=gb[:].rearrange("p t (c i) -> p c t i", i=4), op=ALU.add)
+            parts[b, jh] = (gb, prod)
+
+        def add_parts(engine, b, jh, j0, j1):
+            gb, prod = parts[b, jh]
+            hb = rounded[b, jh]
+            engine.tensor_tensor(
+                out=hb[:, j0 * PACK:j1 * PACK].rearrange("p (c i t) -> p c t i", i=4, t=PACK),
+                in0=prod[:, :, j0:j1].rearrange("p t (c i) -> p c t i", i=4),
+                in1=gb[:, :, j0:j1].rearrange("p t (c i) -> p c t i", i=4), op=ALU.add)
+
+        def quantize_h(b, jh):
             codes = kept([P, NT], U32, "hc%d%d" % (b, jh))
             scales = kept([P, NT], U8, "hs%d%d" % (b, jh))
-            nc.vector.quantize_mx(out=codes[:].bitcast(FP8X4), scales=scales[:], in_=hb[:])
+            nc.vector.quantize_mx(out=codes[:].bitcast(FP8X4), scales=scales[:], in_=rounded[b, jh][:])
             hq[b, jh] = (codes, scales)
 
         e = [kept([P, S], F32, "e%d" % m) for m in range(S2 // P)]
@@ -173,46 +193,63 @@ def tile_list_firework_shell_scores_kernel(
             for b in range(2):
                 codes, scales = hq[b, jh]
                 nc.tensor.matmul_mx(
-                    out=acc_e[:], lhsT=v2w[b, m // 2][:, (m % 2) * P:(m % 2 + 1) * P].bitcast(FP8X4),
+                    out=acc_e[:], lhsT=v2w[m // 2][:, b, (m % 2) * P:(m % 2 + 1) * P].bitcast(FP8X4),
                     lhsT_scale=v2s[4 * b:P, m * P:(m + 1) * P],
                     rhs=codes[:].bitcast(FP8X4), rhs_scale=scales[:], start=(b == 0), stop=(b == 1))
             nc.scalar.activation(out=e[m][:, jh * NT:(jh + 1) * NT], in_=acc_e[:], func=ACT.Abs)
 
-        def gather_v2(mh):
+        def gather_v2(mh, words):
+            v2w[mh] = words
             for b in range(2):
-                nc.vector.tensor_copy(v2w[b, mh][:],
+                nc.vector.tensor_copy(words[:, b, :],
                                       tab2w[b][:].bitcast(U32).indirect(offs2_sb[:, 16 * mh:16 * mh + 16]))
 
-        def finish(m, n0, n1):
-            width = n1 - n0
-            launch = ring.tile([P, width], F32, name="launch")
-            burst = ring.tile([P, width], F32, name="burst")
-            nc.vector.tensor_copy(launch[:], e[m][:].indirect(pos1_sb[:, n0 // 16:n1 // 16]))
-            nc.vector.tensor_copy(burst[:], e[m][:].indirect(pos2_sb[:, n0 // 16:n1 // 16]))
-            larger = ring.tile([P, width], F32, name="larger")
-            nc.vector.tensor_tensor(out=larger[:], in0=launch[:], in1=burst[:], op=ALU.max)
-            result = ring.tile([P, width], F32, name="result")
-            nc.scalar.activation(out=result[:], in_=larger[:], func=ACT.Copy, scale=shell_sb[:, m:m + 1])
-            nc.sync.dma_start(out=out[m * P:(m + 1) * P, n0:n1], in_=result[:])
+        picked = {}
 
-        stage1(0, 0)
-        quantize_w1(1, 0)
-        quantize_w1(1, 1)
-        stage1(0, 1)
-        stage1(1, 0)
-        gather_v2(0)
+        def pick(name, pos_sb, m, n0, n1):
+            tile = ring.tile([P, n1 - n0], F32, name=name)
+            nc.vector.tensor_copy(tile[:], e[m][:].indirect(pos_sb[:, n0 // 16:n1 // 16]))
+            picked[name, m, n0] = tile
+
+        def finish(m, n0, n1):
+            larger = ring.tile([P, n1 - n0], F32, name="larger")
+            nc.vector.tensor_tensor(out=larger[:], in0=picked["launch", m, n0][:], in1=picked["burst", m, n0][:],
+                                    op=ALU.max)
+            result = ring.tile([P, n1 - n0], F32, name="result")
+            nc.scalar.activation(out=result[:], in_=larger[:], func=ACT.Copy, scale=shell_sb[:, m:m + 1])
+            nc.scalar.dma_start(out=out[m * P:(m + 1) * P, n0:n1], in_=result[:])
+
+        def finish_h(b, jh, hb):
+            rounded[b, jh] = hb
+            add_parts(nc.vector, b, jh, 0, NT)
+            quantize_h(b, jh)
+
+        def rounded_tile():
+            return ring.tile([P, NT * PACK], BF16, name="hb", align_bytes=64)
+
+        products(0, 0)
+        products(0, 1)
+        finish_h(0, 0, rounded_tile())
+        for a in range(2):
+            quantize_w1(1, a, ring.tile([P, KP * PACK], BF16, name="w1g", align_bytes=64), on_scalar)
+        products(1, 0)
+        finish_h(0, 1, rounded_tile())
+        products(1, 1)
+        finish_h(1, 0, rounded_tile())
+        gather_v2(0, kept([P, 2, S2 // 2], U32, "v2w0"))
         stage2(0, 0)
         stage2(1, 0)
-        stage1(1, 1)
-        gather_v2(1)
+        finish_h(1, 1, keep.tile([P, NT * PACK], BF16, name="hb_last", tag="last", align_bytes=64))
+        gather_v2(1, keep.tile([P, 2, S2 // 2], U32, name="v2w1", tag="last", align_bytes=64))
         stage2(0, 1)
         stage2(1, 1)
-        finish(0, 0, NP)
-        stage2(2, 0)
-        stage2(2, 1)
-        finish(1, 0, NP)
-        stage2(3, 0)
-        stage2(3, 1)
-        finish(2, 0, NP)
-        finish(3, 0, NP // 2)
-        finish(3, NP // 2, NP)
+        for m in range(2, S2 // P):
+            for jh in range(2):
+                stage2(m, jh)
+        pieces = [(0, 0, NP), (1, 0, NP), (2, 0, NP), (3, 0, NP // 2), (3, NP // 2, NP)]
+        for n, piece in enumerate(pieces):
+            pick("launch", pos1_sb, *piece)
+            if n > 0:
+                finish(*pieces[n - 1])
+            pick("burst", pos2_sb, *piece)
+        finish(*pieces[-1])

from contextlib import ExitStack

import concourse.mybir as mybir

K, H, T, S, T3, S2, NP = 1024, 1024, 4096, 1024, 2048, 512, 512
FLOPS = 2 * K * H * S * 2 + 2 * H * S2 * S

F32 = mybir.dt.float32
BF16 = mybir.dt.bfloat16
I32 = mybir.dt.int32
U32 = mybir.dt.uint32
U16 = mybir.dt.uint16
U8 = mybir.dt.uint8
FP8X4 = mybir.dt.float8_e4m3fn_x4
FP4X4 = mybir.dt.float4_e2m1fn_x4
ACT = mybir.ActivationFunctionType
ALU = mybir.AluOpType

P = 128
PACK = 4
KP = 512
NT = 512
HALF = 256


def tile_list_firework_shell_scores_kernel(
    tc, tab_words, tab_scales, tab2_words, tab2_scales, w1, w4_words, w4_scales,
    gain, shell, offs, offs2, pos1, pos2, out,
):
    nc = tc.nc
    with ExitStack() as ctx:
        keep = ctx.enter_context(tc.tile_pool(name="keep", bufs=1))
        ring = ctx.enter_context(tc.tile_pool(name="ring", bufs=2))
        psum = ctx.enter_context(tc.psum_pool(name="psum", bufs=1))

        def kept(shape, dtype, name):
            return keep.tile(shape, dtype, name=name, align_bytes=64)

        offs_sb = kept([P, S // 16], U16, "offs_sb")
        offs2_sb = kept([P, S2 // 16], U16, "offs2_sb")
        pos1_sb = kept([P, NP // 16], U16, "pos1_sb")
        pos2_sb = kept([P, NP // 16], U16, "pos2_sb")
        tabw = [kept([P, T], I32, "tabw%d" % a) for a in range(2)]
        tabs = kept([P, 2 * T], U8, "tabs")
        tab2w = [kept([P, T3], I32, "tab2w%d" % a) for a in range(2)]
        tab2s = kept([P, T3], U8, "tab2s")
        w4w_raw = kept([P, 2 * 2 * H], U8, "w4w_raw")
        w4s_raw = kept([P, 2 * H], U8, "w4s_raw")
        w4w = kept([P, 2 * 2 * H], U8, "w4w")
        w4s = kept([P, 2 * H], U8, "w4s")
        gain_sb = kept([P, 2, PACK], F32, "gain_sb")
        shell_sb = kept([P, S2 // P], F32, "shell_sb")
        w1raw = {(b, a, ch): keep.tile([P, PACK, HALF], F32, name="w1raw%d%d%d" % (b, a, ch),
                                       tag="w1raw%d%d%d" % (b, a, ch), align_bytes=64)
                 for b in range(2) for a in range(2) for ch in range(2)}

        def load_w1(b, a):
            for ch in range(2):
                c0 = b * KP + ch * HALF
                rows = w1[a * KP:(a + 1) * KP, c0:c0 + HALF]
                nc.sync.dma_start(out=w1raw[b, a, ch][:], in_=rows.rearrange("(p j) c -> p j c", j=PACK))

        def load_words(tile, words):
            nc.sync.dma_start(out=tile, in_=words.rearrange("p t i -> p (t i)").bitcast(I32))

        def load_side_by_side(queue, tile, scales):
            for q in range(4):
                queue.dma_start(
                    out=tile[32 * q:32 * q + 4, :].bitcast(I32).rearrange("r (a c) -> r a c", a=2),
                    in_=scales[:, 4 * q:4 * q + 4, :].bitcast(I32).rearrange("a r c -> r a c"))

        def load_packed(queue, tile, scales):
            for q in range(4):
                queue.dma_start(out=tile[32 * q:32 * q + 8, :].bitcast(I32),
                                in_=scales[:, 4 * q:4 * q + 4, :].bitcast(I32))

        vs = [kept([P, S], U8, "vs%d" % a) for a in range(2)]
        nc.gpsimd.memset(tabs[:, 0:T].bitcast(I32), 0)
        nc.vector.memset(tabs[:, T:2 * T].bitcast(I32), 0)
        nc.gpsimd.memset(w4s_raw[:].bitcast(I32), 0)
        nc.gpsimd.memset(tab2s[:].bitcast(I32), 0)

        nc.sync.dma_start(offs_sb[:], offs)
        nc.sync.dma_start(out=gain_sb[:], in_=gain.rearrange("(b p t) -> p b t", b=2, t=PACK))
        nc.sync.dma_start(out=w4w_raw[:].bitcast(I32).rearrange("p (a c) -> p a c", a=2),
                          in_=w4_words.bitcast(I32).rearrange("a p c -> p a c"))
        load_side_by_side(nc.sync, tabs, tab_scales)
        load_words(tabw[0][:], tab_words[0])
        nc.sync.dma_start(offs2_sb[:], offs2)
        load_packed(nc.gpsimd, tab2s, tab2_scales)
        load_w1(0, 0)
        load_side_by_side(nc.sync, w4s_raw, w4_scales)
        load_words(tabw[1][:], tab_words[1])
        load_w1(0, 1)
        load_w1(1, 0)
        load_w1(1, 1)
        load_words(tab2w[0][:], tab2_words[0])
        load_words(tab2w[1][:], tab2_words[1])
        nc.sync.dma_start(pos1_sb[:], pos1)
        nc.sync.dma_start(pos2_sb[:], pos2)
        with nc.allow_non_contiguous_dma(reason="one factor a partition"):
            nc.sync.dma_start(out=shell_sb[:], in_=shell.rearrange("(m p) -> p m", p=P))

        nc.vector.tensor_copy(
            out=w4w[:].bitcast(U16).rearrange("p (g t m) -> p g m t", t=PACK, m=P),
            in_=w4w_raw[:].bitcast(U16).rearrange("p (g m t) -> p g m t", t=PACK, m=P))

        vw = {(a, jh): kept([P, NT], U32, "vw%d%d" % (a, jh)) for a in range(2) for jh in range(2)}
        v2w = {}
        v2s = kept([P, S2], U8, "v2s")

        def gather_v(a, jh):
            nc.vector.tensor_copy(vw[a, jh][:], tabw[a][:].bitcast(U32).indirect(offs_sb[:, 32 * jh:32 * jh + 32]))

        w1q = {}

        def quantize_w1(b, a, grouped, casts):
            by_channel = grouped[:].rearrange("p (t m j) -> p m j t", t=PACK, j=PACK)
            for ch in range(2):
                casts[ch](out=by_channel[:, ch * 64:(ch + 1) * 64],
                          in_=w1raw[b, a, ch][:].rearrange("p j (m t) -> p m j t", t=PACK))
            codes = keep.tile([P, KP], U32, name="w1c%d%d" % (b, a), tag="w1c%d%d" % (b, a), align_bytes=64)
            scales = kept([P, KP], U8, "w1s%d%d" % (b, a))
            nc.vector.quantize_mx(out=codes[:].bitcast(FP8X4), scales=scales[:], in_=grouped[:])
            w1q[b, a] = (codes, scales)

        for a in range(2):
            nc.vector.tensor_copy(vs[a][:], tabs[:, a * T:(a + 1) * T].indirect(offs_sb[:]))
        gather_v(0, 0)
        gather_v(0, 1)
        nc.vector.tensor_copy(
            out=w4s[:].rearrange("p (g t m) -> p g m t", t=PACK, m=P),
            in_=w4s_raw[:].rearrange("p (g m t) -> p g m t", t=PACK, m=P))
        on_scalar = (nc.scalar.copy, nc.scalar.copy)
        quantize_w1(0, 0, ring.tile([P, KP * PACK], BF16, name="w1g", align_bytes=64), on_scalar)
        nc.vector.tensor_copy(v2s[:], tab2s[:].indirect(offs2_sb[:]))
        gather_v(1, 0)
        gather_v(1, 1)
        quantize_w1(0, 1, keep.tile([P, KP * PACK], BF16, name="w1g01", tag="slot1", align_bytes=64),
                    (nc.scalar.copy, nc.vector.tensor_copy))

        hq = {}
        parts = {}
        rounded = {}
        groups = [(0, 0), (0, 1), (1, 0), (1, 1)]
        gains = {}
        for n, (b, jh) in enumerate(groups):
            gains[b, jh] = keep.tile([P, PACK], F32, name="gains%d" % n, tag="slot%d" % n if n else "w1raw010", align_bytes=64)
            nc.gpsimd.tensor_copy(gains[b, jh][:], gain_sb[:, b, :])

        def products(b, jh):
            gb = ring.tile([P, PACK, NT], F32, name="gb", bufs=3)
            prod = ring.tile([P, PACK, NT], F32, name="prod")
            cols = slice(jh * NT, (jh + 1) * NT)
            for t in range(PACK):
                acc_b = psum.tile([P, NT], F32, name="acc_b", bufs=3)
                acc_a = psum.tile([P, NT], F32, name="acc_a", bufs=3)
                for a in range(2):
                    c0 = a * H + b * KP + t * P
                    nc.tensor.matmul_mx(
                        out=acc_b[:], lhsT=w4w[:, 2 * c0:2 * c0 + 2 * P].bitcast(FP4X4), lhsT_scale=w4s[:, c0:c0 + P],
                        rhs=vw[a, jh][:].bitcast(FP8X4), rhs_scale=vs[a][:, cols], start=(a == 0), stop=(a == 1))
                for a in range(2):
                    codes, scales = w1q[b, a]
                    nc.tensor.matmul_mx(
                        out=acc_a[:], lhsT=codes[:, t * P:(t + 1) * P].bitcast(FP8X4),
                        lhsT_scale=scales[:, t * P:(t + 1) * P],
                        rhs=vw[a, jh][:].bitcast(FP8X4), rhs_scale=vs[a][:, cols], start=(a == 0), stop=(a == 1))
                g = gains[b, jh][:, t:t + 1]
                nc.scalar.activation(out=gb[:, t, :], in_=acc_b[:], func=ACT.Copy, scale=g)
                nc.vector.scalar_tensor_tensor(out=prod[:, t, :], in0=gb[:, t, :], scalar=g, in1=acc_a[:],
                                               op0=ALU.add, op1=ALU.mult)
            parts[b, jh] = (gb, prod)

        def add_parts(engine, b, jh, j0, j1):
            gb, prod = parts[b, jh]
            hb = rounded[b, jh]
            engine.tensor_tensor(
                out=hb[:, j0 * PACK:j1 * PACK].rearrange("p (c i t) -> p c t i", i=4, t=PACK),
                in0=prod[:, :, j0:j1].rearrange("p t (c i) -> p c t i", i=4),
                in1=gb[:, :, j0:j1].rearrange("p t (c i) -> p c t i", i=4), op=ALU.add)

        def quantize_h(b, jh):
            codes = kept([P, NT], U32, "hc%d%d" % (b, jh))
            scales = kept([P, NT], U8, "hs%d%d" % (b, jh))
            nc.vector.quantize_mx(out=codes[:].bitcast(FP8X4), scales=scales[:], in_=rounded[b, jh][:])
            hq[b, jh] = (codes, scales)

        e = [kept([P, S], F32, "e%d" % m) for m in range(S2 // P)]

        def stage2(m, jh):
            acc_e = psum.tile([P, NT], F32, name="acc_e", bufs=2)
            for b in range(2):
                codes, scales = hq[b, jh]
                nc.tensor.matmul_mx(
                    out=acc_e[:], lhsT=v2w[m // 2][:, b, (m % 2) * P:(m % 2 + 1) * P].bitcast(FP8X4),
                    lhsT_scale=v2s[4 * b:P, m * P:(m + 1) * P],
                    rhs=codes[:].bitcast(FP8X4), rhs_scale=scales[:], start=(b == 0), stop=(b == 1))
            nc.scalar.activation(out=e[m][:, jh * NT:(jh + 1) * NT], in_=acc_e[:], func=ACT.Abs)

        def gather_v2(mh, words):
            v2w[mh] = words
            for b in range(2):
                nc.vector.tensor_copy(words[:, b, :],
                                      tab2w[b][:].bitcast(U32).indirect(offs2_sb[:, 16 * mh:16 * mh + 16]))

        picked = {}

        def pick(name, pos_sb, m, n0, n1):
            tile = ring.tile([P, n1 - n0], F32, name=name)
            nc.vector.tensor_copy(tile[:], e[m][:].indirect(pos_sb[:, n0 // 16:n1 // 16]))
            picked[name, m, n0] = tile

        def finish(m, n0, n1):
            larger = ring.tile([P, n1 - n0], F32, name="larger")
            nc.vector.tensor_tensor(out=larger[:], in0=picked["launch", m, n0][:], in1=picked["burst", m, n0][:],
                                    op=ALU.max)
            result = ring.tile([P, n1 - n0], F32, name="result")
            nc.scalar.activation(out=result[:], in_=larger[:], func=ACT.Copy, scale=shell_sb[:, m:m + 1])
            nc.scalar.dma_start(out=out[m * P:(m + 1) * P, n0:n1], in_=result[:])

        def finish_h(b, jh, hb):
            rounded[b, jh] = hb
            add_parts(nc.vector, b, jh, 0, NT)
            quantize_h(b, jh)

        def rounded_tile():
            return ring.tile([P, NT * PACK], BF16, name="hb", align_bytes=64)

        products(0, 0)
        products(0, 1)
        finish_h(0, 0, rounded_tile())
        for a in range(2):
            quantize_w1(1, a, ring.tile([P, KP * PACK], BF16, name="w1g", align_bytes=64), on_scalar)
        products(1, 0)
        finish_h(0, 1, rounded_tile())
        products(1, 1)
        finish_h(1, 0, rounded_tile())
        gather_v2(0, kept([P, 2, S2 // 2], U32, "v2w0"))
        stage2(0, 0)
        stage2(1, 0)
        finish_h(1, 1, keep.tile([P, NT * PACK], BF16, name="hb_last", tag="last", align_bytes=64))
        gather_v2(1, keep.tile([P, 2, S2 // 2], U32, name="v2w1", tag="last", align_bytes=64))
        stage2(0, 1)
        stage2(1, 1)
        for m in range(2, S2 // P):
            for jh in range(2):
                stage2(m, jh)
        pieces = [(0, 0, NP), (1, 0, NP), (2, 0, NP), (3, 0, NP // 2), (3, NP // 2, NP)]
        for n, piece in enumerate(pieces):
            pick("launch", pos1_sb, *piece)
            if n > 0:
                finish(*pieces[n - 1])
            pick("burst", pos2_sb, *piece)
        finish(*pieces[-1])
